import numpy as np
import ml_dtypes


def mxq(x, axis, fmt="e4m3"):
    dtype, down = {"e4m3": (ml_dtypes.float8_e4m3fn, 7), "e5m2": (ml_dtypes.float8_e5m2, 14)}[fmt]
    v = np.moveaxis(np.asarray(x, np.float32).astype(ml_dtypes.bfloat16).astype(np.float64), axis, -1)
    blocks = v.reshape(v.shape[:-1] + (-1, 32))
    amax = np.abs(blocks).max(-1, keepdims=True)
    byte = np.maximum(np.where(amax > 0, np.frexp(amax)[1] - 1 + 127, 0) - down, 1)
    scale = np.exp2(byte - 127.0)
    codes = (blocks / scale).astype(np.float32).astype(dtype).astype(np.float64)
    return np.moveaxis((codes * scale).reshape(v.shape), -1, axis)


WIDE = False


def mx_kscale(k):
    if not WIDE:
        return np.ones(k)
    levels = np.array([10, -10, 5, -5, 0])
    if k % 512:
        return np.exp2(np.random.permutation(np.resize(levels, k // 32))).repeat(32)
    a = np.empty((k // 512, 16))
    for p in range(k // 512):
        a[p, :8] = np.random.permutation(np.resize(levels, 8))
        for g in range(8):
            far = levels[np.abs(levels - a[p, g]) >= 10]
            a[p, g + 8] = far[np.random.randint(len(far))]
    return np.exp2(a.ravel()).repeat(32)


def f64(x):
    return np.asarray(x).astype(np.float64)


def striped(idx):
    return np.tile(idx.reshape(-1, 16).T, (8, 1)).astype(np.uint16)


def unstriped(offs):
    return offs[:16].T.reshape(-1).astype(np.int64)


def pack_weight(w):
    k, n = w.shape
    w = f64(np.asarray(w, np.float32).astype(ml_dtypes.bfloat16)).reshape(k // 32, 32, n)
    amax = np.abs(w).max(1)
    byte = np.clip(np.where(amax > 0, np.frexp(amax)[1] - 1 + 127 - 7, 1), 1, 254)
    scaled = (w * np.exp2(127.0 - byte)[:, None, :]).reshape(k, n).astype(np.float32)
    words = np.ascontiguousarray(scaled.reshape(k // 512, 128, 4, n).transpose(0, 1, 3, 2)).astype(ml_dtypes.float8_e4m3fn).view(np.uint8)
    return words, np.ascontiguousarray(byte.astype(np.uint8).reshape(k // 512, 16, n))


def unpack_weight(words, scales):
    g, p, n, _ = words.shape
    vals = np.ascontiguousarray(words).view(ml_dtypes.float8_e4m3fn).astype(np.float64) * np.repeat(np.exp2(scales.astype(np.float64) - 127.0), 8, axis=1)[..., None]
    return vals.transpose(0, 1, 3, 2).reshape(g * 512, n)


K, T, S, N = 512, 1024, 512, 128
P = 2 ** 7


def setup_inputs():
    n = np.random.standard_normal
    s = mx_kscale(K)[:, None]
    packed_xT = pack_weight(n((K, T)) * s)
    return {
        "x_words": packed_xT[0],
        "x_scales": packed_xT[1],
        "w1": (n((K, N)) / np.sqrt(K) / s).astype(np.float32),
        "flow": (np.random.uniform(0.2, 2.0, (N, S))).astype(np.float32),
        "infl": (np.random.uniform(0.2, 2.0, (N, S))).astype(np.float32),
        "cou": (np.tile(np.random.uniform(0.2, 0.8, S), (P, 1))).astype(np.float32),
        "offs": striped(np.random.permutation(T)[:S]),
        "tra": striped(np.random.permutation(S)),
        "trb": striped(np.random.permutation(S)),
    }


def reference(x_words, x_scales, w1, flow, infl, cou, offs, tra, trb):
    xq = unpack_weight(x_words, x_scales)[:, unstriped(offs)]
    y = mxq(f64(w1), 0, "e4m3").T @ xq
    lat = np.log(np.exp(y) + 1.0)
    oa = (f64(cou)[:1] * lat + f64(cou)[:1] * f64(infl) + (-1.0 * (0.5 * f64(cou)[:1]) + 1.0) * f64(flow)) / (1.5 * f64(cou)[:1] + 1.0)
    ib = 0.6 * (oa[:, unstriped(tra)] + oa[:, unstriped(trb)]) + 0.3 * lat
    return (f64(cou)[:1] * ib + f64(cou)[:1] * lat + (-1.0 * (0.5 * f64(cou)[:1]) + 1.0) * oa) / (1.5 * f64(cou)[:1] + 1.0)

@@ -1,0 +1,144 @@
+from contextlib import ExitStack
+
+import concourse.mybir as mybir
+from concourse.masks import make_identity
+
+K, T, S, N = 512, 1024, 512, 128
+FLOPS = 2 * K * N * S
+
+F32 = mybir.dt.float32
+BF16 = mybir.dt.bfloat16
+I32 = mybir.dt.int32
+U32 = mybir.dt.uint32
+U16 = mybir.dt.uint16
+U8 = mybir.dt.uint8
+FP8X4 = mybir.dt.float8_e4m3fn_x4
+ALU = mybir.AluOpType
+ACT = mybir.ActivationFunctionType
+
+P = 128
+PACK = 4
+HALF = S // 2
+KAPPA = 0.6 / 1.3
+EXP_CAP = 2.0**60
+
+
+def tile_picked_ymuskr_flow_p_kernel(tc, x_words, x_scales, w1, flow, infl, cou, offs, tra, trb, out):
+    nc = tc.nc
+    halves = [slice(h * HALF, (h + 1) * HALF) for h in range(2)]
+    list_halves = [slice(h * HALF // 16, (h + 1) * HALF // 16) for h in range(2)]
+
+    with ExitStack() as ctx:
+        lists = ctx.enter_context(tc.tile_pool(name="lists", bufs=1))
+        sb = ctx.enter_context(tc.tile_pool(name="sb", bufs=1))
+        psum = ctx.enter_context(tc.psum_pool(name="psum", bufs=1))
+
+        offs_sb = lists.tile([P, S // 16], U16, name="offs_sb")
+        tra_sb = lists.tile([P, S // 16], U16, name="tra_sb")
+        trb_sb = lists.tile([P, S // 16], U16, name="trb_sb")
+
+        scale_table = sb.tile([P, T], U8, name="scale_table", align_bytes=64)
+        word_table = sb.tile([P, T], I32, name="word_table", align_bytes=64)
+        w_raw = sb.tile([P, PACK, N], F32, name="w_raw", align_bytes=64)
+        cou4 = sb.tile([P, PACK], F32, name="cou4")
+        flow_sb = sb.tile([P, S], F32, name="flow_sb", align_bytes=64)
+        infl_sb = sb.tile([P, S], F32, name="infl_sb", align_bytes=64)
+
+        nc.sync.dma_start(offs_sb[:], offs)
+        scale_rows = x_scales[0].bitcast(I32)
+        for q in range(4):
+            nc.scalar.dma_start(
+                scale_table[32 * q : 32 * (q + 1), :].bitcast(I32),
+                scale_rows[4 * q : 4 * q + 4, :].unsqueeze(0).to_broadcast([8, 4, T // 4]),
+            )
+        nc.scalar.dma_start(cou4[:], cou[0].rearrange("(p t) -> p t", t=PACK))
+        nc.sync.dma_start(w_raw[:], w1.rearrange("(p j) n -> p j n", j=PACK))
+        nc.sync.dma_start(word_table[:], x_words[0].rearrange("p n t -> p (n t)").bitcast(I32))
+        nc.sync.dma_start(flow_sb[:], flow)
+        nc.sync.dma_start(infl_sb[:], infl)
+        nc.sync.dma_start(tra_sb[:], tra)
+        nc.sync.dma_start(trb_sb[:], trb)
+
+        ident = sb.tile([P, P], F32, name="ident", align_bytes=64)
+        make_identity(nc, ident[:])
+
+        x_scale = sb.tile([P, S], U8, name="x_scale", align_bytes=64)
+        nc.vector.tensor_copy(x_scale[:], scale_table[:].indirect(offs_sb[:]))
+
+        den4 = sb.tile([P, PACK], F32, name="den4")
+        rec4 = sb.tile([P, PACK], F32, name="rec4")
+        a4 = sb.tile([P, PACK], F32, name="a4")
+        nc.vector.tensor_scalar(den4[:], cou4[:], 1.5, 1.0, ALU.mult, ALU.add)
+        nc.vector.reciprocal(rec4[:], den4[:])
+        nc.vector.scalar_tensor_tensor(a4[:], cou4[:], KAPPA, rec4[:], ALU.mult, ALU.mult)
+        a_ps = psum.tile([P, S], F32, name="a_ps")
+        a_by_t = a_ps[:].rearrange("m (q t) -> m t q", t=PACK)
+        for t in range(PACK):
+            nc.tensor.transpose(a_by_t[:, t, :], a4[:, t : t + 1].to_broadcast([P, P]), ident[:])
+
+        w_bf = sb.tile([P, N, PACK], BF16, name="w_bf", align_bytes=64)
+        nc.scalar.activation(w_bf[:], w_raw[:].rearrange("p j n -> p n j"), ACT.Copy)
+        w_codes = sb.tile([P, N], U32, name="w_codes", align_bytes=64)
+        w_scale = sb.tile([P, N], U8, name="w_scale", align_bytes=64)
+        nc.vector.quantize_mx(
+            out=w_codes[:].bitcast(FP8X4), scales=w_scale[:], in_=w_bf[:].rearrange("p n j -> p (n j)")
+        )
+
+        exp_y = sb.tile([P, S], F32, name="exp_y", align_bytes=64)
+        y_ps = []
+        for h in range(2):
+            x_codes = sb.tile([P, HALF], U32, name="x_codes%d" % h, align_bytes=64)
+            nc.vector.tensor_copy(x_codes[:], word_table[:].bitcast(U32).indirect(offs_sb[:, list_halves[h]]))
+            y = psum.tile([P, HALF], F32, name="y%d" % h)
+            nc.tensor.matmul_mx(
+                out=y[:],
+                lhsT=w_codes[:].bitcast(FP8X4),
+                lhsT_scale=w_scale[:],
+                rhs=x_codes[:].bitcast(FP8X4),
+                rhs_scale=x_scale[:, halves[h]],
+                start=True,
+                stop=True,
+            )
+            nc.scalar.activation(exp_y[:, halves[h]], y[:], ACT.Exp)
+            y_ps.append(y)
+
+        warm = sb.tile([P, 1], F32, name="warm")
+        nc.scalar.activation(warm[:], exp_y[:, S - 1 : S], ACT.Ln)
+
+        diff = sb.tile([P, S], F32, name="diff", align_bytes=64)
+        nc.vector.scalar_tensor_tensor(diff[:], flow_sb[:], -2.0, infl_sb[:], ALU.mult, ALU.add)
+        a_diff = sb.tile([P, S], F32, name="a_diff", align_bytes=64)
+        nc.vector.tensor_tensor(a_diff[:], diff[:], a_ps[:], ALU.mult)
+        exp1 = sb.tile([P, S], F32, name="exp1", align_bytes=64)
+        nc.vector.tensor_scalar(exp1[:], exp_y[:], EXP_CAP, 1.0, ALU.min, ALU.add)
+        base = sb.tile([P, S], F32, name="base", align_bytes=64)
+        nc.vector.scalar_tensor_tensor(base[:], flow_sb[:], KAPPA, a_diff[:], ALU.mult, ALU.add)
+
+        log1 = sb.tile([P, S], F32, name="log1", align_bytes=64)
+        lat = sb.tile([P, S], F32, name="lat", align_bytes=64)
+        a_lat = sb.tile([P, S], F32, name="a_lat", align_bytes=64)
+        oa = sb.tile([P, S], F32, name="oa", align_bytes=64)
+        own = sb.tile([P, S], F32, name="own", align_bytes=64)
+        sum_a = sb.tile([P, S], F32, name="sum_a", align_bytes=64)
+        sum_b = sb.tile([P, S], F32, name="sum_b", align_bytes=64)
+        step = sb.tile([P, S], F32, name="step", align_bytes=64)
+        res = sb.tile([P, S], F32, name="res", align_bytes=64)
+        for c in halves:
+            nc.scalar.activation(log1[:, c], exp1[:, c], ACT.Ln)
+        for h, c in enumerate(halves):
+            nc.vector.tensor_tensor(lat[:, c], y_ps[h][:], log1[:, c], ALU.max)
+        for c in halves:
+            nc.vector.tensor_tensor(a_lat[:, c], lat[:, c], a_ps[:, c], ALU.mult)
+        for c in halves:
+            nc.vector.tensor_tensor(oa[:, c], a_lat[:, c], base[:, c], ALU.add)
+        for c in halves:
+            nc.vector.scalar_tensor_tensor(own[:, c], oa[:, c], -2.0 / 0.6, lat[:, c], ALU.mult, ALU.add)
+        for h, c in enumerate(halves):
+            nc.vector.tensor_tensor(sum_a[:, c], oa[:].indirect(tra_sb[:, list_halves[h]]), own[:, c], ALU.add)
+        for h, c in enumerate(halves):
+            nc.vector.tensor_tensor(sum_b[:, c], oa[:].indirect(trb_sb[:, list_halves[h]]), sum_a[:, c], ALU.add)
+        for c in halves:
+            nc.vector.scalar_tensor_tensor(step[:, c], sum_b[:, c], 1.3 / KAPPA, a_ps[:, c], ALU.mult, ALU.mult)
+        for c in halves:
+            nc.vector.scalar_tensor_tensor(res[:, c], oa[:, c], 1.0 / KAPPA, step[:, c], ALU.mult, ALU.add)
+            nc.sync.dma_start(out[:, c], res[:, c])

@@ -26,6 +26,7 @@ EXP_CAP = 2.0**60
 def tile_picked_ymuskr_flow_p_kernel(tc, x_words, x_scales, w1, flow, infl, cou, offs, tra, trb, out):
     nc = tc.nc
     halves = [slice(h * HALF, (h + 1) * HALF) for h in range(2)]
+    pieces = [slice(0, 256), slice(256, 384), slice(384, 512)]
     list_halves = [slice(h * HALF // 16, (h + 1) * HALF // 16) for h in range(2)]
 
     with ExitStack() as ctx:
@@ -38,7 +39,7 @@ def tile_picked_ymuskr_flow_p_kernel(tc, x_words, x_scales, w1, flow, infl, cou,
         trb_sb = lists.tile([P, S // 16], U16, name="trb_sb")
 
         scale_table = sb.tile([P, T], U8, name="scale_table", align_bytes=64)
-        word_table = sb.tile([P, T], I32, name="word_table", align_bytes=64)
+        word_table = sb.tile([P, T], I32, name="word_table", tag="words_then_diff", align_bytes=64)
         w_raw = sb.tile([P, PACK, N], F32, name="w_raw", align_bytes=64)
         cou4 = sb.tile([P, PACK], F32, name="cou4")
         flow_sb = sb.tile([P, S], F32, name="flow_sb", align_bytes=64)
@@ -47,11 +48,11 @@ def tile_picked_ymuskr_flow_p_kernel(tc, x_words, x_scales, w1, flow, infl, cou,
         nc.sync.dma_start(offs_sb[:], offs)
         scale_rows = x_scales[0].bitcast(I32)
         for q in range(4):
-            nc.scalar.dma_start(
+            (nc.sync if q < 2 else nc.scalar).dma_start(
                 scale_table[32 * q : 32 * (q + 1), :].bitcast(I32),
                 scale_rows[4 * q : 4 * q + 4, :].unsqueeze(0).to_broadcast([8, 4, T // 4]),
             )
-        nc.scalar.dma_start(cou4[:], cou[0].rearrange("(p t) -> p t", t=PACK))
+        nc.sync.dma_start(cou4[:], cou[0].rearrange("(p t) -> p t", t=PACK))
         nc.sync.dma_start(w_raw[:], w1.rearrange("(p j) n -> p j n", j=PACK))
         nc.sync.dma_start(word_table[:], x_words[0].rearrange("p n t -> p (n t)").bitcast(I32))
         nc.sync.dma_start(flow_sb[:], flow)
@@ -62,21 +63,24 @@ def tile_picked_ymuskr_flow_p_kernel(tc, x_words, x_scales, w1, flow, infl, cou,
         ident = sb.tile([P, P], F32, name="ident", align_bytes=64)
         make_identity(nc, ident[:])
 
-        x_scale = sb.tile([P, S], U8, name="x_scale", align_bytes=64)
-        nc.vector.tensor_copy(x_scale[:], scale_table[:].indirect(offs_sb[:]))
+        x_scale0 = sb.tile([P, HALF], U8, name="x_scale0", align_bytes=64)
+        nc.vector.tensor_copy(x_scale0[:], scale_table[:].indirect(offs_sb[:, list_halves[0]]))
 
-        den4 = sb.tile([P, PACK], F32, name="den4")
+        den4 = sb.tile([P, PACK], F32, name="den4", tag="den_then_scale", align_bytes=64)
         rec4 = sb.tile([P, PACK], F32, name="rec4")
         a4 = sb.tile([P, PACK], F32, name="a4")
-        nc.vector.tensor_scalar(den4[:], cou4[:], 1.5, 1.0, ALU.mult, ALU.add)
+        nc.gpsimd.tensor_scalar(den4[:], cou4[:], 1.5 / KAPPA, 1.0 / KAPPA, ALU.mult, ALU.add)
         nc.vector.reciprocal(rec4[:], den4[:])
-        nc.vector.scalar_tensor_tensor(a4[:], cou4[:], KAPPA, rec4[:], ALU.mult, ALU.mult)
+        x_scale1 = sb.tile([P, HALF], U8, name="x_scale1", tag="den_then_scale", align_bytes=64)
+        nc.vector.tensor_copy(x_scale1[:], scale_table[:].indirect(offs_sb[:, list_halves[1]]))
+        x_scale = [x_scale0[:], x_scale1[:, : HALF // 2], x_scale1[:, HALF // 2 :]]
+        nc.gpsimd.tensor_tensor(a4[:], cou4[:], rec4[:], ALU.mult)
         a_ps = psum.tile([P, S], F32, name="a_ps")
         a_by_t = a_ps[:].rearrange("m (q t) -> m t q", t=PACK)
         for t in range(PACK):
             nc.tensor.transpose(a_by_t[:, t, :], a4[:, t : t + 1].to_broadcast([P, P]), ident[:])
 
-        w_bf = sb.tile([P, N, PACK], BF16, name="w_bf", align_bytes=64)
+        w_bf = sb.tile([P, N, PACK], BF16, name="w_bf", tag="w_bf_then_codes", align_bytes=64)
         nc.scalar.activation(w_bf[:], w_raw[:].rearrange("p j n -> p n j"), ACT.Copy)
         w_codes = sb.tile([P, N], U32, name="w_codes", align_bytes=64)
         w_scale = sb.tile([P, N], U8, name="w_scale", align_bytes=64)
@@ -86,26 +90,25 @@ def tile_picked_ymuskr_flow_p_kernel(tc, x_words, x_scales, w1, flow, infl, cou,
 
         exp_y = sb.tile([P, S], F32, name="exp_y", align_bytes=64)
         y_ps = []
-        for h in range(2):
-            x_codes = sb.tile([P, HALF], U32, name="x_codes%d" % h, align_bytes=64)
-            nc.vector.tensor_copy(x_codes[:], word_table[:].bitcast(U32).indirect(offs_sb[:, list_halves[h]]))
-            y = psum.tile([P, HALF], F32, name="y%d" % h)
+        x_codes = sb.tile([P, S], U32, name="x_codes", tag="w_bf_then_codes", align_bytes=64)
+        for i, c in enumerate(pieces):
+            width = c.stop - c.start
+            nc.vector.tensor_copy(x_codes[:, c], word_table[:].bitcast(U32).indirect(offs_sb[:, c.start // 16 : c.stop // 16]))
+            y = psum.tile([P, width], F32, name="y%d" % i)
             nc.tensor.matmul_mx(
                 out=y[:],
                 lhsT=w_codes[:].bitcast(FP8X4),
                 lhsT_scale=w_scale[:],
-                rhs=x_codes[:].bitcast(FP8X4),
-                rhs_scale=x_scale[:, halves[h]],
+                rhs=x_codes[:, c].bitcast(FP8X4),
+                rhs_scale=x_scale[i],
                 start=True,
                 stop=True,
             )
-            nc.scalar.activation(exp_y[:, halves[h]], y[:], ACT.Exp)
+            nc.scalar.activation(exp_y[:, c], y[:], ACT.Exp)
             y_ps.append(y)
 
-        warm = sb.tile([P, 1], F32, name="warm")
-        nc.scalar.activation(warm[:], exp_y[:, S - 1 : S], ACT.Ln)
 
-        diff = sb.tile([P, S], F32, name="diff", align_bytes=64)
+        diff = sb.tile([P, S], F32, name="diff", tag="words_then_diff", align_bytes=64)
         nc.vector.scalar_tensor_tensor(diff[:], flow_sb[:], -2.0, infl_sb[:], ALU.mult, ALU.add)
         a_diff = sb.tile([P, S], F32, name="a_diff", align_bytes=64)
         nc.vector.tensor_tensor(a_diff[:], diff[:], a_ps[:], ALU.mult)
@@ -123,10 +126,12 @@ def tile_picked_ymuskr_flow_p_kernel(tc, x_words, x_scales, w1, flow, infl, cou,
         sum_b = sb.tile([P, S], F32, name="sum_b", align_bytes=64)
         step = sb.tile([P, S], F32, name="step", align_bytes=64)
         res = sb.tile([P, S], F32, name="res", align_bytes=64)
-        for c in halves:
+        for i in (1, 2, 0):
+            c = pieces[i]
             nc.scalar.activation(log1[:, c], exp1[:, c], ACT.Ln)
-        for h, c in enumerate(halves):
-            nc.vector.tensor_tensor(lat[:, c], y_ps[h][:], log1[:, c], ALU.max)
+            nc.vector.tensor_tensor(lat[:, c], y_ps[i][:], log1[:, c], ALU.max)
+        halves = halves[::-1]
+        list_halves = list_halves[::-1]
         for c in halves:
             nc.vector.tensor_tensor(a_lat[:, c], lat[:, c], a_ps[:, c], ALU.mult)
         for c in halves:

@@ -67,7 +67,7 @@ def tile_picked_ymuskr_flow_p_kernel(tc, x_words, x_scales, w1, flow, infl, cou,
         nc.vector.tensor_copy(x_scale0[:], scale_table[:].indirect(offs_sb[:, list_halves[0]]))
 
         den4 = sb.tile([P, PACK], F32, name="den4", tag="den_then_scale", align_bytes=64)
-        rec4 = sb.tile([P, PACK], F32, name="rec4")
+        rec4 = sb.tile([P, PACK], F32, name="rec4", tag="rec_then_scale", align_bytes=64)
         a4 = sb.tile([P, PACK], F32, name="a4")
         nc.gpsimd.tensor_scalar(den4[:], cou4[:], 1.5 / KAPPA, 1.0 / KAPPA, ALU.mult, ALU.add)
         nc.vector.reciprocal(rec4[:], den4[:])
@@ -75,6 +75,8 @@ def tile_picked_ymuskr_flow_p_kernel(tc, x_words, x_scales, w1, flow, infl, cou,
         nc.vector.tensor_copy(x_scale1[:], scale_table[:].indirect(offs_sb[:, list_halves[1]]))
         x_scale = [x_scale0[:], x_scale1[:, : HALF // 2], x_scale1[:, HALF // 2 :]]
         nc.gpsimd.tensor_tensor(a4[:], cou4[:], rec4[:], ALU.mult)
+        b4 = sb.tile([P, PACK], F32, name="b4")
+        nc.gpsimd.tensor_scalar(b4[:], a4[:], -2.0 / KAPPA**2, 1.0 / KAPPA, ALU.mult, ALU.add)
         a_ps = psum.tile([P, S], F32, name="a_ps")
         a_by_t = a_ps[:].rearrange("m (q t) -> m t q", t=PACK)
         for t in range(PACK):
@@ -83,7 +85,7 @@ def tile_picked_ymuskr_flow_p_kernel(tc, x_words, x_scales, w1, flow, infl, cou,
         w_bf = sb.tile([P, N, PACK], BF16, name="w_bf", tag="w_bf_then_codes", align_bytes=64)
         nc.scalar.activation(w_bf[:], w_raw[:].rearrange("p j n -> p n j"), ACT.Copy)
         w_codes = sb.tile([P, N], U32, name="w_codes", align_bytes=64)
-        w_scale = sb.tile([P, N], U8, name="w_scale", align_bytes=64)
+        w_scale = sb.tile([P, N], U8, name="w_scale", tag="rec_then_scale", align_bytes=64)
         nc.vector.quantize_mx(
             out=w_codes[:].bitcast(FP8X4), scales=w_scale[:], in_=w_bf[:].rearrange("p n j -> p (n j)")
         )
@@ -94,7 +96,7 @@ def tile_picked_ymuskr_flow_p_kernel(tc, x_words, x_scales, w1, flow, infl, cou,
         for i, c in enumerate(pieces):
             width = c.stop - c.start
             nc.vector.tensor_copy(x_codes[:, c], word_table[:].bitcast(U32).indirect(offs_sb[:, c.start // 16 : c.stop // 16]))
-            y = psum.tile([P, width], F32, name="y%d" % i)
+            y = psum.tile([P, width], F32, name="y%d" % i, tag="turned%d" % i)
             nc.tensor.matmul_mx(
                 out=y[:],
                 lhsT=w_codes[:].bitcast(FP8X4),
@@ -121,7 +123,6 @@ def tile_picked_ymuskr_flow_p_kernel(tc, x_words, x_scales, w1, flow, infl, cou,
         lat = sb.tile([P, S], F32, name="lat", align_bytes=64)
         a_lat = sb.tile([P, S], F32, name="a_lat", align_bytes=64)
         oa = sb.tile([P, S], F32, name="oa", align_bytes=64)
-        own = sb.tile([P, S], F32, name="own", align_bytes=64)
         sum_a = sb.tile([P, S], F32, name="sum_a", align_bytes=64)
         sum_b = sb.tile([P, S], F32, name="sum_b", align_bytes=64)
         step = sb.tile([P, S], F32, name="step", align_bytes=64)
@@ -136,14 +137,22 @@ def tile_picked_ymuskr_flow_p_kernel(tc, x_words, x_scales, w1, flow, infl, cou,
             nc.vector.tensor_tensor(a_lat[:, c], lat[:, c], a_ps[:, c], ALU.mult)
         for c in halves:
             nc.vector.tensor_tensor(oa[:, c], a_lat[:, c], base[:, c], ALU.add)
-        for c in halves:
-            nc.vector.scalar_tensor_tensor(own[:, c], oa[:, c], -2.0 / 0.6, lat[:, c], ALU.mult, ALU.add)
+        kept_ps = psum.tile([P, S], F32, name="kept_ps")
+        kept_by_t = kept_ps[:].rearrange("m (q t) -> m t q", t=PACK)
+        oa_by_t = oa[:].rearrange("m (q t) -> m t q", t=PACK)
+        kept_t = sb.tile([P, PACK, P], F32, name="kept_t", align_bytes=64)
+        for t in range(PACK):
+            turned = psum.tile([P, P], F32, name="turned%d" % t, tag="turned%d" % t)
+            nc.tensor.transpose(turned[:], oa_by_t[:, t, :], ident[:])
+            nc.scalar.activation(kept_t[:, t, :], turned[:], ACT.Copy, scale=b4[:, t : t + 1])
+        for t in range(PACK):
+            nc.tensor.transpose(kept_by_t[:, t, :], kept_t[:, t, :], ident[:])
         for h, c in enumerate(halves):
-            nc.vector.tensor_tensor(sum_a[:, c], oa[:].indirect(tra_sb[:, list_halves[h]]), own[:, c], ALU.add)
+            nc.vector.tensor_tensor(sum_a[:, c], oa[:].indirect(tra_sb[:, list_halves[h]]), lat[:, c], ALU.add)
         for h, c in enumerate(halves):
             nc.vector.tensor_tensor(sum_b[:, c], oa[:].indirect(trb_sb[:, list_halves[h]]), sum_a[:, c], ALU.add)
         for c in halves:
             nc.vector.scalar_tensor_tensor(step[:, c], sum_b[:, c], 1.3 / KAPPA, a_ps[:, c], ALU.mult, ALU.mult)
         for c in halves:
-            nc.vector.scalar_tensor_tensor(res[:, c], oa[:, c], 1.0 / KAPPA, step[:, c], ALU.mult, ALU.add)
+            nc.vector.tensor_tensor(res[:, c], step[:, c], kept_ps[:, c], ALU.add)
             nc.sync.dma_start(out[:, c], res[:, c])

@@ -1,3 +1,4 @@
+import math
 from contextlib import ExitStack
 
 import concourse.mybir as mybir
@@ -20,7 +21,9 @@ P = 128
 PACK = 4
 HALF = S // 2
 KAPPA = 0.6 / 1.3
-EXP_CAP = 2.0**60
+Y_CAP = 22.0
+EXP_CAP = math.exp(Y_CAP)
+GAIN = 1.3 / KAPPA
 
 
 def tile_picked_ymuskr_flow_p_kernel(tc, x_words, x_scales, w1, flow, infl, cou, offs, tra, trb, out):
@@ -63,6 +66,9 @@ def tile_picked_ymuskr_flow_p_kernel(tc, x_words, x_scales, w1, flow, infl, cou,
         ident = sb.tile([P, P], F32, name="ident", align_bytes=64)
         make_identity(nc, ident[:])
 
+        y_cap = sb.tile([P, 1], F32, name="y_cap", tag="cap_exp1_over", align_bytes=64)
+        nc.gpsimd.memset(y_cap[:], Y_CAP)
+
         x_scale0 = sb.tile([P, HALF], U8, name="x_scale0", align_bytes=64)
         nc.vector.tensor_copy(x_scale0[:], scale_table[:].indirect(offs_sb[:, list_halves[0]]))
 
@@ -76,7 +82,6 @@ def tile_picked_ymuskr_flow_p_kernel(tc, x_words, x_scales, w1, flow, infl, cou,
         x_scale = [x_scale0[:], x_scale1[:, : HALF // 2], x_scale1[:, HALF // 2 :]]
         nc.gpsimd.tensor_tensor(a4[:], cou4[:], rec4[:], ALU.mult)
         b4 = sb.tile([P, PACK], F32, name="b4")
-        nc.gpsimd.tensor_scalar(b4[:], a4[:], -2.0 / KAPPA**2, 1.0 / KAPPA, ALU.mult, ALU.add)
         a_ps = psum.tile([P, S], F32, name="a_ps")
         a_by_t = a_ps[:].rearrange("m (q t) -> m t q", t=PACK)
         for t in range(PACK):
@@ -84,6 +89,11 @@ def tile_picked_ymuskr_flow_p_kernel(tc, x_words, x_scales, w1, flow, infl, cou,
 
         w_bf = sb.tile([P, N, PACK], BF16, name="w_bf", tag="w_bf_then_codes", align_bytes=64)
         nc.scalar.activation(w_bf[:], w_raw[:].rearrange("p j n -> p n j"), ACT.Copy)
+        ka4 = sb.tile([P, PACK], F32, name="ka4")
+        kc4 = sb.tile([P, PACK], F32, name="kc4")
+        nc.scalar.activation(b4[:], a4[:], ACT.Copy, bias=1.0 / KAPPA, scale=-2.0 / KAPPA**2)
+        nc.scalar.activation(ka4[:], a4[:], ACT.Copy, scale=GAIN)
+        nc.scalar.activation(kc4[:], a4[:], ACT.Copy, scale=-GAIN * Y_CAP)
         w_codes = sb.tile([P, N], U32, name="w_codes", align_bytes=64)
         w_scale = sb.tile([P, N], U8, name="w_scale", tag="rec_then_scale", align_bytes=64)
         nc.vector.quantize_mx(
@@ -110,35 +120,54 @@ def tile_picked_ymuskr_flow_p_kernel(tc, x_words, x_scales, w1, flow, infl, cou,
             y_ps.append(y)
 
 
-        diff = sb.tile([P, S], F32, name="diff", tag="words_then_diff", align_bytes=64)
-        nc.vector.scalar_tensor_tensor(diff[:], flow_sb[:], -2.0, infl_sb[:], ALU.mult, ALU.add)
-        a_diff = sb.tile([P, S], F32, name="a_diff", align_bytes=64)
-        nc.vector.tensor_tensor(a_diff[:], diff[:], a_ps[:], ALU.mult)
-        exp1 = sb.tile([P, S], F32, name="exp1", align_bytes=64)
+        lack = sb.tile([P, S], F32, name="lack", tag="words_then_diff", align_bytes=64)
+        for c in halves:
+            nc.vector.scalar_tensor_tensor(lack[:, c], flow_sb[:, c], 2.0, infl_sb[:, c], ALU.mult, ALU.subtract)
+        gross = sb.tile([P, S], F32, name="gross", align_bytes=64)
+        for i, c in enumerate(pieces):
+            nc.vector.scalar_tensor_tensor(
+                gross[:, c], y_ps[i][:], y_cap[:] if i == 0 else Y_CAP, lack[:, c], ALU.max, ALU.subtract
+            )
+        exp1 = sb.tile([P, S], F32, name="exp1", tag="cap_exp1_over", align_bytes=64)
         nc.vector.tensor_scalar(exp1[:], exp_y[:], EXP_CAP, 1.0, ALU.min, ALU.add)
+        a_net = sb.tile([P, S], F32, name="a_net", align_bytes=64)
         base = sb.tile([P, S], F32, name="base", align_bytes=64)
-        nc.vector.scalar_tensor_tensor(base[:], flow_sb[:], KAPPA, a_diff[:], ALU.mult, ALU.add)
+        for c in halves:
+            nc.vector.scalar_tensor_tensor(a_net[:, c], gross[:, c], -Y_CAP, a_ps[:, c], ALU.add, ALU.mult)
+        for c in halves:
+            nc.vector.scalar_tensor_tensor(base[:, c], flow_sb[:, c], KAPPA, a_net[:, c], ALU.mult, ALU.add)
+
+        ymax_ps = psum.tile([P, PACK, P], F32, name="ymax_ps")
+        for s, src in enumerate((lack, gross)):
+            src_by_t = src[:].rearrange("m (q t) -> m t q", t=PACK)
+            for t in range(PACK):
+                nc.tensor.matmul(
+                    ymax_ps[:, t, :], src_by_t[:, t, :], ident[:], is_transpose=True,
+                    start=(s == 0 and t == 0), stop=(s == 1 and t == PACK - 1),
+                )
 
         log1 = sb.tile([P, S], F32, name="log1", align_bytes=64)
-        lat = sb.tile([P, S], F32, name="lat", align_bytes=64)
-        a_lat = sb.tile([P, S], F32, name="a_lat", align_bytes=64)
+        a_log = sb.tile([P, S], F32, name="a_log", align_bytes=64)
         oa = sb.tile([P, S], F32, name="oa", align_bytes=64)
         sum_a = sb.tile([P, S], F32, name="sum_a", align_bytes=64)
         sum_b = sb.tile([P, S], F32, name="sum_b", align_bytes=64)
         step = sb.tile([P, S], F32, name="step", align_bytes=64)
         res = sb.tile([P, S], F32, name="res", align_bytes=64)
-        for i in (1, 2, 0):
-            c = pieces[i]
+        for c in halves:
             nc.scalar.activation(log1[:, c], exp1[:, c], ACT.Ln)
-            nc.vector.tensor_tensor(lat[:, c], y_ps[i][:], log1[:, c], ALU.max)
-        halves = halves[::-1]
-        list_halves = list_halves[::-1]
         for c in halves:
-            nc.vector.tensor_tensor(a_lat[:, c], lat[:, c], a_ps[:, c], ALU.mult)
+            nc.vector.tensor_tensor(a_log[:, c], log1[:, c], a_ps[:, c], ALU.mult)
         for c in halves:
-            nc.vector.tensor_tensor(oa[:, c], a_lat[:, c], base[:, c], ALU.add)
+            nc.vector.tensor_tensor(oa[:, c], a_log[:, c], base[:, c], ALU.add)
+
         kept_ps = psum.tile([P, S], F32, name="kept_ps")
         kept_by_t = kept_ps[:].rearrange("m (q t) -> m t q", t=PACK)
+        over_t = sb.tile([P, PACK, P], F32, name="over_t", tag="cap_exp1_over", align_bytes=64)
+        for t in range(PACK):
+            nc.scalar.activation(
+                over_t[:, t, :], ymax_ps[:, t, :], ACT.Identity, scale=ka4[:, t : t + 1], bias=kc4[:, t : t + 1]
+            )
+            nc.tensor.matmul(kept_by_t[:, t, :], over_t[:, t, :], ident[:], is_transpose=True, start=(t == 0), stop=False)
         oa_by_t = oa[:].rearrange("m (q t) -> m t q", t=PACK)
         kept_t = sb.tile([P, PACK, P], F32, name="kept_t", align_bytes=64)
         for t in range(PACK):
@@ -146,13 +175,15 @@ def tile_picked_ymuskr_flow_p_kernel(tc, x_words, x_scales, w1, flow, infl, cou,
             nc.tensor.transpose(turned[:], oa_by_t[:, t, :], ident[:])
             nc.scalar.activation(kept_t[:, t, :], turned[:], ACT.Copy, scale=b4[:, t : t + 1])
         for t in range(PACK):
-            nc.tensor.transpose(kept_by_t[:, t, :], kept_t[:, t, :], ident[:])
+            nc.tensor.matmul(
+                kept_by_t[:, t, :], kept_t[:, t, :], ident[:], is_transpose=True, start=False, stop=(t == PACK - 1)
+            )
         for h, c in enumerate(halves):
-            nc.vector.tensor_tensor(sum_a[:, c], oa[:].indirect(tra_sb[:, list_halves[h]]), lat[:, c], ALU.add)
+            nc.vector.tensor_tensor(sum_a[:, c], oa[:].indirect(tra_sb[:, list_halves[h]]), log1[:, c], ALU.add)
         for h, c in enumerate(halves):
             nc.vector.tensor_tensor(sum_b[:, c], oa[:].indirect(trb_sb[:, list_halves[h]]), sum_a[:, c], ALU.add)
         for c in halves:
-            nc.vector.scalar_tensor_tensor(step[:, c], sum_b[:, c], 1.3 / KAPPA, a_ps[:, c], ALU.mult, ALU.mult)
+            nc.vector.scalar_tensor_tensor(step[:, c], sum_b[:, c], GAIN, a_ps[:, c], ALU.mult, ALU.mult)
         for c in halves:
             nc.vector.tensor_tensor(res[:, c], step[:, c], kept_ps[:, c], ALU.add)
             nc.sync.dma_start(out[:, c], res[:, c])

@@ -35,6 +35,7 @@ def tile_picked_ymuskr_flow_p_kernel(tc, x_words, x_scales, w1, flow, infl, cou,
     with ExitStack() as ctx:
         lists = ctx.enter_context(tc.tile_pool(name="lists", bufs=1))
         sb = ctx.enter_context(tc.tile_pool(name="sb", bufs=1))
+        early = ctx.enter_context(tc.tile_pool(name="early", bufs=1))
         psum = ctx.enter_context(tc.psum_pool(name="psum", bufs=1))
 
         offs_sb = lists.tile([P, S // 16], U16, name="offs_sb")
@@ -48,6 +49,7 @@ def tile_picked_ymuskr_flow_p_kernel(tc, x_words, x_scales, w1, flow, infl, cou,
         flow_sb = sb.tile([P, S], F32, name="flow_sb", align_bytes=64)
         infl_sb = sb.tile([P, S], F32, name="infl_sb", align_bytes=64)
 
+        nc.sync.dma_start(cou4[:], cou[0].rearrange("(p t) -> p t", t=PACK))
         nc.sync.dma_start(offs_sb[:], offs)
         scale_rows = x_scales[0].bitcast(I32)
         for q in range(4):
@@ -55,11 +57,11 @@ def tile_picked_ymuskr_flow_p_kernel(tc, x_words, x_scales, w1, flow, infl, cou,
                 scale_table[32 * q : 32 * (q + 1), :].bitcast(I32),
                 scale_rows[4 * q : 4 * q + 4, :].unsqueeze(0).to_broadcast([8, 4, T // 4]),
             )
-        nc.sync.dma_start(cou4[:], cou[0].rearrange("(p t) -> p t", t=PACK))
         nc.sync.dma_start(w_raw[:], w1.rearrange("(p j) n -> p j n", j=PACK))
         nc.sync.dma_start(word_table[:], x_words[0].rearrange("p n t -> p (n t)").bitcast(I32))
-        nc.sync.dma_start(flow_sb[:], flow)
-        nc.sync.dma_start(infl_sb[:], infl)
+        for c in halves:
+            nc.sync.dma_start(flow_sb[:, c], flow[:, c])
+            nc.sync.dma_start(infl_sb[:, c], infl[:, c])
         nc.sync.dma_start(tra_sb[:], tra)
         nc.sync.dma_start(trb_sb[:], trb)
 
@@ -69,15 +71,18 @@ def tile_picked_ymuskr_flow_p_kernel(tc, x_words, x_scales, w1, flow, infl, cou,
         y_cap = sb.tile([P, 1], F32, name="y_cap", tag="cap_exp1_over", align_bytes=64)
         nc.gpsimd.memset(y_cap[:], Y_CAP)
 
+        slope = early.tile([P, 256], F32, name="slope", offset=0, align_bytes=64)
+        nc.gpsimd.memset(slope[:, 0:1], 3.25)
+
         x_scale0 = sb.tile([P, HALF], U8, name="x_scale0", align_bytes=64)
         nc.vector.tensor_copy(x_scale0[:], scale_table[:].indirect(offs_sb[:, list_halves[0]]))
 
-        den4 = sb.tile([P, PACK], F32, name="den4", tag="den_then_scale", align_bytes=64)
-        rec4 = sb.tile([P, PACK], F32, name="rec4", tag="rec_then_scale", align_bytes=64)
+        den4 = sb.tile([P, PACK], F32, name="den4")
+        rec4 = sb.tile([P, PACK], F32, name="rec4")
         a4 = sb.tile([P, PACK], F32, name="a4")
-        nc.gpsimd.tensor_scalar(den4[:], cou4[:], 1.5 / KAPPA, 1.0 / KAPPA, ALU.mult, ALU.add)
+        nc.gpsimd.tensor_scalar(den4[:], cou4[:], slope[:, 0:1], 1.0 / KAPPA, ALU.mult, ALU.add)
         nc.vector.reciprocal(rec4[:], den4[:])
-        x_scale1 = sb.tile([P, HALF], U8, name="x_scale1", tag="den_then_scale", align_bytes=64)
+        x_scale1 = early.tile([P, HALF], U8, name="x_scale1", offset=0, align_bytes=64)
         nc.vector.tensor_copy(x_scale1[:], scale_table[:].indirect(offs_sb[:, list_halves[1]]))
         x_scale = [x_scale0[:], x_scale1[:, : HALF // 2], x_scale1[:, HALF // 2 :]]
         nc.gpsimd.tensor_tensor(a4[:], cou4[:], rec4[:], ALU.mult)
@@ -87,7 +92,7 @@ def tile_picked_ymuskr_flow_p_kernel(tc, x_words, x_scales, w1, flow, infl, cou,
         for t in range(PACK):
             nc.tensor.transpose(a_by_t[:, t, :], a4[:, t : t + 1].to_broadcast([P, P]), ident[:])
 
-        w_bf = sb.tile([P, N, PACK], BF16, name="w_bf", tag="w_bf_then_codes", align_bytes=64)
+        w_bf = sb.tile([P, N, PACK], BF16, name="w_bf", align_bytes=64)
         nc.scalar.activation(w_bf[:], w_raw[:].rearrange("p j n -> p n j"), ACT.Copy)
         ka4 = sb.tile([P, PACK], F32, name="ka4")
         kc4 = sb.tile([P, PACK], F32, name="kc4")
@@ -95,14 +100,14 @@ def tile_picked_ymuskr_flow_p_kernel(tc, x_words, x_scales, w1, flow, infl, cou,
         nc.scalar.activation(ka4[:], a4[:], ACT.Copy, scale=GAIN)
         nc.scalar.activation(kc4[:], a4[:], ACT.Copy, scale=-GAIN * Y_CAP)
         w_codes = sb.tile([P, N], U32, name="w_codes", align_bytes=64)
-        w_scale = sb.tile([P, N], U8, name="w_scale", tag="rec_then_scale", align_bytes=64)
+        w_scale = early.tile([P, N], U8, name="w_scale", offset=256, align_bytes=64)
         nc.vector.quantize_mx(
             out=w_codes[:].bitcast(FP8X4), scales=w_scale[:], in_=w_bf[:].rearrange("p n j -> p (n j)")
         )
 
         exp_y = sb.tile([P, S], F32, name="exp_y", align_bytes=64)
         y_ps = []
-        x_codes = sb.tile([P, S], U32, name="x_codes", tag="w_bf_then_codes", align_bytes=64)
+        x_codes = early.tile([P, S], U32, name="x_codes", offset=512, align_bytes=64)
         for i, c in enumerate(pieces):
             width = c.stop - c.start
             nc.vector.tensor_copy(x_codes[:, c], word_table[:].bitcast(U32).indirect(offs_sb[:, c.start // 16 : c.stop // 16]))

import math
from contextlib import ExitStack

import concourse.mybir as mybir
from concourse.masks import make_identity

K, T, S, N = 512, 1024, 512, 128
FLOPS = 2 * K * N * S

F32 = mybir.dt.float32
BF16 = mybir.dt.bfloat16
I32 = mybir.dt.int32
U32 = mybir.dt.uint32
U16 = mybir.dt.uint16
U8 = mybir.dt.uint8
FP8X4 = mybir.dt.float8_e4m3fn_x4
ALU = mybir.AluOpType
ACT = mybir.ActivationFunctionType

P = 128
PACK = 4
HALF = S // 2
KAPPA = 0.6 / 1.3
Y_CAP = 22.0
EXP_CAP = math.exp(Y_CAP)
GAIN = 1.3 / KAPPA


def tile_picked_ymuskr_flow_p_kernel(tc, x_words, x_scales, w1, flow, infl, cou, offs, tra, trb, out):
    nc = tc.nc
    halves = [slice(h * HALF, (h + 1) * HALF) for h in range(2)]
    pieces = [slice(0, 256), slice(256, 384), slice(384, 512)]
    list_halves = [slice(h * HALF // 16, (h + 1) * HALF // 16) for h in range(2)]

    with ExitStack() as ctx:
        lists = ctx.enter_context(tc.tile_pool(name="lists", bufs=1))
        sb = ctx.enter_context(tc.tile_pool(name="sb", bufs=1))
        early = ctx.enter_context(tc.tile_pool(name="early", bufs=1))
        psum = ctx.enter_context(tc.psum_pool(name="psum", bufs=1))

        offs_sb = lists.tile([P, S // 16], U16, name="offs_sb")
        tra_sb = lists.tile([P, S // 16], U16, name="tra_sb")
        trb_sb = lists.tile([P, S // 16], U16, name="trb_sb")

        scale_table = sb.tile([P, T], U8, name="scale_table", align_bytes=64)
        word_table = sb.tile([P, T], I32, name="word_table", tag="words_then_diff", align_bytes=64)
        w_raw = sb.tile([P, PACK, N], F32, name="w_raw", align_bytes=64)
        cou4 = sb.tile([P, PACK], F32, name="cou4")
        flow_sb = sb.tile([P, S], F32, name="flow_sb", align_bytes=64)
        infl_sb = sb.tile([P, S], F32, name="infl_sb", align_bytes=64)

        nc.sync.dma_start(cou4[:], cou[0].rearrange("(p t) -> p t", t=PACK))
        nc.sync.dma_start(offs_sb[:], offs)
        scale_rows = x_scales[0].bitcast(I32)
        for q in range(4):
            (nc.sync if q < 2 else nc.scalar).dma_start(
                scale_table[32 * q : 32 * (q + 1), :].bitcast(I32),
                scale_rows[4 * q : 4 * q + 4, :].unsqueeze(0).to_broadcast([8, 4, T // 4]),
            )
        nc.sync.dma_start(w_raw[:], w1.rearrange("(p j) n -> p j n", j=PACK))
        nc.sync.dma_start(word_table[:], x_words[0].rearrange("p n t -> p (n t)").bitcast(I32))
        for c in halves:
            nc.sync.dma_start(flow_sb[:, c], flow[:, c])
            nc.sync.dma_start(infl_sb[:, c], infl[:, c])
        nc.sync.dma_start(tra_sb[:], tra)
        nc.sync.dma_start(trb_sb[:], trb)

        ident = sb.tile([P, P], F32, name="ident", align_bytes=64)
        make_identity(nc, ident[:])

        y_cap = sb.tile([P, 1], F32, name="y_cap", tag="cap_exp1_over", align_bytes=64)
        nc.gpsimd.memset(y_cap[:], Y_CAP)

        slope = early.tile([P, 256], F32, name="slope", offset=0, align_bytes=64)
        nc.gpsimd.memset(slope[:, 0:1], 3.25)

        x_scale0 = sb.tile([P, HALF], U8, name="x_scale0", align_bytes=64)
        nc.vector.tensor_copy(x_scale0[:], scale_table[:].indirect(offs_sb[:, list_halves[0]]))

        den4 = sb.tile([P, PACK], F32, name="den4")
        rec4 = sb.tile([P, PACK], F32, name="rec4")
        a4 = sb.tile([P, PACK], F32, name="a4")
        nc.gpsimd.tensor_scalar(den4[:], cou4[:], slope[:, 0:1], 1.0 / KAPPA, ALU.mult, ALU.add)
        nc.vector.reciprocal(rec4[:], den4[:])
        x_scale1 = early.tile([P, HALF], U8, name="x_scale1", offset=0, align_bytes=64)
        nc.vector.tensor_copy(x_scale1[:], scale_table[:].indirect(offs_sb[:, list_halves[1]]))
        x_scale = [x_scale0[:], x_scale1[:, : HALF // 2], x_scale1[:, HALF // 2 :]]
        nc.gpsimd.tensor_tensor(a4[:], cou4[:], rec4[:], ALU.mult)
        b4 = sb.tile([P, PACK], F32, name="b4")
        a_ps = psum.tile([P, S], F32, name="a_ps")
        a_by_t = a_ps[:].rearrange("m (q t) -> m t q", t=PACK)
        for t in range(PACK):
            nc.tensor.transpose(a_by_t[:, t, :], a4[:, t : t + 1].to_broadcast([P, P]), ident[:])

        w_bf = sb.tile([P, N, PACK], BF16, name="w_bf", align_bytes=64)
        nc.scalar.activation(w_bf[:], w_raw[:].rearrange("p j n -> p n j"), ACT.Copy)
        ka4 = sb.tile([P, PACK], F32, name="ka4")
        kc4 = sb.tile([P, PACK], F32, name="kc4")
        nc.scalar.activation(b4[:], a4[:], ACT.Copy, bias=1.0 / KAPPA, scale=-2.0 / KAPPA**2)
        nc.scalar.activation(ka4[:], a4[:], ACT.Copy, scale=GAIN)
        nc.scalar.activation(kc4[:], a4[:], ACT.Copy, scale=-GAIN * Y_CAP)
        w_codes = sb.tile([P, N], U32, name="w_codes", align_bytes=64)
        w_scale = early.tile([P, N], U8, name="w_scale", offset=256, align_bytes=64)
        nc.vector.quantize_mx(
            out=w_codes[:].bitcast(FP8X4), scales=w_scale[:], in_=w_bf[:].rearrange("p n j -> p (n j)")
        )

        exp_y = sb.tile([P, S], F32, name="exp_y", align_bytes=64)
        y_ps = []
        x_codes = early.tile([P, S], U32, name="x_codes", offset=512, align_bytes=64)
        for i, c in enumerate(pieces):
            width = c.stop - c.start
            nc.vector.tensor_copy(x_codes[:, c], word_table[:].bitcast(U32).indirect(offs_sb[:, c.start // 16 : c.stop // 16]))
            y = psum.tile([P, width], F32, name="y%d" % i, tag="turned%d" % i)
            nc.tensor.matmul_mx(
                out=y[:],
                lhsT=w_codes[:].bitcast(FP8X4),
                lhsT_scale=w_scale[:],
                rhs=x_codes[:, c].bitcast(FP8X4),
                rhs_scale=x_scale[i],
                start=True,
                stop=True,
            )
            nc.scalar.activation(exp_y[:, c], y[:], ACT.Exp)
            y_ps.append(y)


        lack = sb.tile([P, S], F32, name="lack", tag="words_then_diff", align_bytes=64)
        for c in halves:
            nc.vector.scalar_tensor_tensor(lack[:, c], flow_sb[:, c], 2.0, infl_sb[:, c], ALU.mult, ALU.subtract)
        gross = sb.tile([P, S], F32, name="gross", align_bytes=64)
        for i, c in enumerate(pieces):
            nc.vector.scalar_tensor_tensor(
                gross[:, c], y_ps[i][:], y_cap[:] if i == 0 else Y_CAP, lack[:, c], ALU.max, ALU.subtract
            )
        exp1 = sb.tile([P, S], F32, name="exp1", tag="cap_exp1_over", align_bytes=64)
        nc.vector.tensor_scalar(exp1[:], exp_y[:], EXP_CAP, 1.0, ALU.min, ALU.add)
        a_net = sb.tile([P, S], F32, name="a_net", align_bytes=64)
        base = sb.tile([P, S], F32, name="base", align_bytes=64)
        for c in halves:
            nc.vector.scalar_tensor_tensor(a_net[:, c], gross[:, c], -Y_CAP, a_ps[:, c], ALU.add, ALU.mult)
        for c in halves:
            nc.vector.scalar_tensor_tensor(base[:, c], flow_sb[:, c], KAPPA, a_net[:, c], ALU.mult, ALU.add)

        ymax_ps = psum.tile([P, PACK, P], F32, name="ymax_ps")
        for s, src in enumerate((lack, gross)):
            src_by_t = src[:].rearrange("m (q t) -> m t q", t=PACK)
            for t in range(PACK):
                nc.tensor.matmul(
                    ymax_ps[:, t, :], src_by_t[:, t, :], ident[:], is_transpose=True,
                    start=(s == 0 and t == 0), stop=(s == 1 and t == PACK - 1),
                )

        log1 = sb.tile([P, S], F32, name="log1", align_bytes=64)
        a_log = sb.tile([P, S], F32, name="a_log", align_bytes=64)
        oa = sb.tile([P, S], F32, name="oa", align_bytes=64)
        sum_a = sb.tile([P, S], F32, name="sum_a", align_bytes=64)
        sum_b = sb.tile([P, S], F32, name="sum_b", align_bytes=64)
        step = sb.tile([P, S], F32, name="step", align_bytes=64)
        res = sb.tile([P, S], F32, name="res", align_bytes=64)
        for c in halves:
            nc.scalar.activation(log1[:, c], exp1[:, c], ACT.Ln)
        for c in halves:
            nc.vector.tensor_tensor(a_log[:, c], log1[:, c], a_ps[:, c], ALU.mult)
        for c in halves:
            nc.vector.tensor_tensor(oa[:, c], a_log[:, c], base[:, c], ALU.add)

        kept_ps = psum.tile([P, S], F32, name="kept_ps")
        kept_by_t = kept_ps[:].rearrange("m (q t) -> m t q", t=PACK)
        over_t = sb.tile([P, PACK, P], F32, name="over_t", tag="cap_exp1_over", align_bytes=64)
        for t in range(PACK):
            nc.scalar.activation(
                over_t[:, t, :], ymax_ps[:, t, :], ACT.Identity, scale=ka4[:, t : t + 1], bias=kc4[:, t : t + 1]
            )
            nc.tensor.matmul(kept_by_t[:, t, :], over_t[:, t, :], ident[:], is_transpose=True, start=(t == 0), stop=False)
        oa_by_t = oa[:].rearrange("m (q t) -> m t q", t=PACK)
        kept_t = sb.tile([P, PACK, P], F32, name="kept_t", align_bytes=64)
        for t in range(PACK):
            turned = psum.tile([P, P], F32, name="turned%d" % t, tag="turned%d" % t)
            nc.tensor.transpose(turned[:], oa_by_t[:, t, :], ident[:])
            nc.scalar.activation(kept_t[:, t, :], turned[:], ACT.Copy, scale=b4[:, t : t + 1])
        for t in range(PACK):
            nc.tensor.matmul(
                kept_by_t[:, t, :], kept_t[:, t, :], ident[:], is_transpose=True, start=False, stop=(t == PACK - 1)
            )
        for h, c in enumerate(halves):
            nc.vector.tensor_tensor(sum_a[:, c], oa[:].indirect(tra_sb[:, list_halves[h]]), log1[:, c], ALU.add)
        for h, c in enumerate(halves):
            nc.vector.tensor_tensor(sum_b[:, c], oa[:].indirect(trb_sb[:, list_halves[h]]), sum_a[:, c], ALU.add)
        for c in halves:
            nc.vector.scalar_tensor_tensor(step[:, c], sum_b[:, c], GAIN, a_ps[:, c], ALU.mult, ALU.mult)
        for c in halves:
            nc.vector.tensor_tensor(res[:, c], step[:, c], kept_ps[:, c], ALU.add)
            nc.sync.dma_start(out[:, c], res[:, c])
